import numpy as np
import ml_dtypes


def mxq(x, axis, fmt="e4m3"):
    dtype, down = {"e4m3": (ml_dtypes.float8_e4m3fn, 7), "e5m2": (ml_dtypes.float8_e5m2, 14)}[fmt]
    v = np.moveaxis(np.asarray(x, np.float32).astype(ml_dtypes.bfloat16).astype(np.float64), axis, -1)
    blocks = v.reshape(v.shape[:-1] + (-1, 32))
    amax = np.abs(blocks).max(-1, keepdims=True)
    byte = np.maximum(np.where(amax > 0, np.frexp(amax)[1] - 1 + 127, 0) - down, 1)
    scale = np.exp2(byte - 127.0)
    codes = (blocks / scale).astype(np.float32).astype(dtype).astype(np.float64)
    return np.moveaxis((codes * scale).reshape(v.shape), -1, axis)


WIDE = False


def mx_kscale(k):
    if not WIDE:
        return np.ones(k)
    levels = np.array([10, -10, 5, -5, 0])
    if k % 512:
        return np.exp2(np.random.permutation(np.resize(levels, k // 32))).repeat(32)
    a = np.empty((k // 512, 16))
    for p in range(k // 512):
        a[p, :8] = np.random.permutation(np.resize(levels, 8))
        for g in range(8):
            far = levels[np.abs(levels - a[p, g]) >= 10]
            a[p, g + 8] = far[np.random.randint(len(far))]
    return np.exp2(a.ravel()).repeat(32)


def f64(x):
    return np.asarray(x).astype(np.float64)


def striped(idx):
    return np.tile(idx.reshape(-1, 16).T, (8, 1)).astype(np.uint16)


def unstriped(offs):
    return offs[:16].T.reshape(-1).astype(np.int64)


def striped8(idx):
    return np.concatenate([x.reshape(-1, 16).T for x in idx]).astype(np.uint16)


def runs(offs, k):
    lists = np.stack([offs[16 * r : 16 * r + 16].T.reshape(-1) for r in range(8)]).astype(np.int64)
    return lists[np.arange(k) % 512 // 64]


def pack_weight(w):
    k, n = w.shape
    w = f64(np.asarray(w, np.float32).astype(ml_dtypes.bfloat16)).reshape(k // 32, 32, n)
    amax = np.abs(w).max(1)
    byte = np.clip(np.where(amax > 0, np.frexp(amax)[1] - 1 + 127 - 7, 1), 1, 254)
    scaled = (w * np.exp2(127.0 - byte)[:, None, :]).reshape(k, n).astype(np.float32)
    words = np.ascontiguousarray(scaled.reshape(k // 512, 128, 4, n).transpose(0, 1, 3, 2)).astype(ml_dtypes.float8_e4m3fn).view(np.uint8)
    return words, np.ascontiguousarray(byte.astype(np.uint8).reshape(k // 512, 16, n))


def unpack_weight(words, scales):
    g, p, n, _ = words.shape
    vals = np.ascontiguousarray(words).view(ml_dtypes.float8_e4m3fn).astype(np.float64) * np.repeat(np.exp2(scales.astype(np.float64) - 127.0), 8, axis=1)[..., None]
    return vals.transpose(0, 1, 3, 2).reshape(g * 512, n)


K, T, S, V, H = 512, 2048, 512, 512, 512


def setup_inputs():
    n = np.random.standard_normal
    s = mx_kscale(K)[:, None]
    u = mx_kscale(S)
    packed_xT = pack_weight(n((K, T)) * s)
    return {
        "x_words": packed_xT[0],
        "x_scales": packed_xT[1],
        "w1": (n((K, H)) / np.sqrt(K) / s).astype(np.float32),
        "w2": (n((K, H)) / np.sqrt(K) / s).astype(np.float32),
        "ga": (np.random.uniform(0.5, 1.5, (H, 1)) * u[:, None]).astype(np.float32),
        "gb": (np.random.uniform(0.5, 1.5, (H, 1)) / u[:, None]).astype(np.float32),
        "offs": striped(np.random.permutation(T)[:S]),
        "two": striped(np.random.permutation(T)[:V]),
        "n1": striped8(np.stack([np.random.permutation(S) for _ in range(8)])),
        "c1": striped8(np.stack([np.random.permutation(V) for _ in range(8)])),
        "c2": striped8(np.stack([np.random.permutation(V) for _ in range(8)])),
    }


def reference(x_words, x_scales, w1, w2, ga, gb, offs, two, n1, c1, c2):
    xq = unpack_weight(x_words, x_scales)[:, unstriped(offs)]
    a = mxq(f64(w1), 0, "e4m3").T @ xq
    z = f64(ga) * (a + 0.5 * (a[np.arange(H)[:, None], runs(n1, H)]))
    x_two = unpack_weight(x_words, x_scales)[:, unstriped(two)]
    b = mxq(f64(w2), 0, "e4m3").T @ x_two
    z2 = f64(gb) * b
    s = 0.0625 * ((mxq(z, 0, "e4m3").T @ mxq(z2, 0, "e4m3")))
    ex = np.exp(0.5 * s)
    return ex / (ex + ex[np.arange(S)[:, None], runs(c1, S)] + ex[np.arange(S)[:, None], runs(c2, S)])

@@ -1,0 +1,188 @@
+from contextlib import ExitStack
+
+import concourse.mybir as mybir
+
+F32 = mybir.dt.float32
+BF16 = mybir.dt.bfloat16
+I32 = mybir.dt.int32
+U32 = mybir.dt.uint32
+U16 = mybir.dt.uint16
+U8 = mybir.dt.uint8
+FP8X4 = mybir.dt.float8_e4m3fn_x4
+ACT = mybir.ActivationFunctionType
+ALU = mybir.AluOpType
+
+P = 128
+PACK = 4
+T = 2048
+N = 512
+HALF = N // 2
+FLOPS = 3 * 2 * 512 * 512 * 512
+
+
+def deal_views(dst, src, m0, m1):
+    d = dst[:].rearrange("p (t m j) -> p m j t", t=PACK, j=PACK)[:, m0:m1]
+    s = src.rearrange("p j (m t) -> p m j t", t=PACK)
+    return d, s
+
+
+def tile_picked_keylsm_none_p_kernel(
+    tc, x_words, x_scales, w1, w2, ga, gb, offs, two, n1, c1, c2, out
+):
+    nc = tc.nc
+    with ExitStack() as ctx:
+        sb = ctx.enter_context(tc.tile_pool(name="sb", bufs=1))
+        ps = ctx.enter_context(tc.psum_pool(name="ps", bufs=1))
+
+        def list_tile(name):
+            return sb.tile([P, N // 16], U16, name=name)
+
+        offs_t, two_t, n1_t, c1_t, c2_t = [list_tile(n) for n in ("offs_t", "two_t", "n1_t", "c1_t", "c2_t")]
+        xw = sb.tile([P, T], U32, name="xw")
+        xs = sb.tile([P, T], U8, name="xs")
+        w1_raw = [sb.tile([P, PACK, HALF], F32, name="w1_raw%d" % h) for h in range(2)]
+        w2_raw = [sb.tile([P, PACK, HALF], F32, name="w2_raw%d" % h) for h in range(2)]
+        ga_t = sb.tile([P, PACK], F32, name="ga_t")
+        gb_t = sb.tile([P, PACK], F32, name="gb_t")
+        ga_half = sb.tile([P, PACK], F32, name="ga_half")
+        a_win = [sb.tile([P, 2 * N], F32, name="a_win%d" % t) for t in range(PACK)]
+        ex_win = [sb.tile([P, 2 * N], F32, name="ex_win%d" % t) for t in range(PACK)]
+
+        s_win = sb.tile([P, 2 * N], F32, name="s_win", tag="s_win")
+        nc.vector.memset(xs[:].bitcast(I32), 0)
+
+        def load_w(dst, w, h):
+            nc.sync.dma_start(out=dst[h][:], in_=w.rearrange("(p j) c -> p j c", j=PACK)[:, :, h * HALF : (h + 1) * HALF])
+
+        nc.sync.dma_start(offs_t[:], offs)
+        nc.sync.dma_start(two_t[:], two)
+        nc.sync.dma_start(out=xw[:].bitcast(I32), in_=x_words[0].rearrange("p n t -> p (n t)").bitcast(I32))
+        for q in range(4):
+            nc.sync.dma_start(out=xs[32 * q : 32 * q + 4, :].bitcast(I32), in_=x_scales[0, 4 * q : 4 * q + 4, :].bitcast(I32))
+        load_w(w1_raw, w1, 0)
+        load_w(w1_raw, w1, 1)
+        nc.sync.dma_start(out=ga_t[:], in_=ga.rearrange("(p t) o -> p (t o)", t=PACK))
+        load_w(w2_raw, w2, 0)
+        load_w(w2_raw, w2, 1)
+        nc.sync.dma_start(n1_t[:], n1)
+        nc.sync.dma_start(out=gb_t[:], in_=gb.rearrange("(p t) o -> p (t o)", t=PACK))
+        nc.sync.dma_start(c1_t[:], c1)
+        nc.sync.dma_start(c2_t[:], c2)
+
+        for t in range(PACK):
+            nc.vector.memset(a_win[t][:, N:], 0.0)
+            nc.gpsimd.memset(ex_win[t][:, N:], 0.0)
+        nc.gpsimd.memset(s_win[:, N:], 0.0)
+        nc.gpsimd.tensor_scalar(ga_half[:], ga_t[:], 0.5, 0.0, ALU.mult, ALU.add)
+
+        def mx_tiles(name):
+            codes = sb.tile([P, N], U32, name=name + "_codes", align_bytes=64)
+            scales = sb.tile([P, N], U8, name=name + "_scales", align_bytes=64)
+            return codes, scales
+
+        def bf_tile(name):
+            return sb.tile([P, PACK * N], BF16, name=name, tag=name, align_bytes=64)
+
+        def quantize(mx, src, c0=0, c1=N):
+            nc.vector.quantize_mx(
+                out=mx[0][:, c0:c1].bitcast(FP8X4), scales=mx[1][:, c0:c1], in_=src[:, PACK * c0 : PACK * c1]
+            )
+
+        def product(bank, stat, t, mov):
+            cols = slice(P * t, P * (t + 1))
+            nc.tensor.matmul_mx(
+                out=bank[:],
+                lhsT=stat[0][:, cols].bitcast(FP8X4),
+                lhsT_scale=stat[1][:, cols],
+                rhs=mov[0][:].bitcast(FP8X4),
+                rhs_scale=mov[1][:],
+                start=True,
+                stop=True,
+            )
+
+        xa, w1q, w2q, zq, z2q = [mx_tiles(n) for n in ("xa", "w1q", "w2q", "zq", "z2q")]
+        w1_bf, w2_bf, z2_bf = [bf_tile(n) for n in ("w1_bf", "w2_bf", "z2_bf")]
+        xb_codes = sb.tile([P, N], U32, name="xb_codes", align_bytes=64)
+
+        nc.vector.tensor_copy(xa[0][:], xw[:].indirect(offs_t[:]))
+        nc.vector.tensor_copy(xa[1][:], xs[:].indirect(offs_t[:]))
+        for h in range(2):
+            d, s = deal_views(w1_bf, w1_raw[h][:], 64 * h, 64 * (h + 1))
+            nc.scalar.copy(d, s)
+        nc.vector.tensor_copy(xb_codes[:], xw[:].indirect(two_t[:]))
+        quantize(w1q, w1_bf, 0, P)
+        quantize(w1q, w1_bf, P, 2 * P)
+        quantize(w1q, w1_bf, 2 * P, N)
+        xb = (xb_codes, sb.tile([P, N], U8, name="xb_scales", tag="w1_bf", align_bytes=64))
+        nc.vector.tensor_copy(xb[1][:], xs[:].indirect(two_t[:]))
+        d, s = deal_views(w2_bf, w2_raw[0][:], 0, 64)
+        nc.scalar.copy(d, s)
+        d, s = deal_views(w2_bf, w2_raw[1][:], 64, 128)
+        nc.vector.tensor_copy(d, s)
+        quantize(w2q, w2_bf)
+
+        a_ps = [ps.tile([P, N], F32, name="a_ps%d" % t, tag="lo%d" % t) for t in range(PACK)]
+        b_ps = [ps.tile([P, N], F32, name="b_ps%d" % t, tag="hi%d" % t) for t in range(PACK)]
+        a_own = [sb.tile([P, N], F32, name="a_own%d" % t) for t in range(PACK)]
+        z32 = sb.tile([P, PACK, N], F32, name="z32")
+        for t in range(PACK):
+            product(a_ps[t], w1q, t, xa)
+            nc.scalar.activation(a_win[t][:, :N], a_ps[t][:], ACT.Copy, scale=ga_half[:, t : t + 1])
+            nc.scalar.activation(a_own[t][:], a_ps[t][:], ACT.Copy, scale=ga_t[:, t : t + 1])
+            nc.vector.tensor_tensor(z32[:, t, :], a_win[t][:].indirect(n1_t[:]), a_own[t][:], ALU.add)
+        z2_planes = sb.tile([P, PACK, N], BF16, name="z2_planes")
+        for t in range(PACK):
+            product(b_ps[t], w2q, t, xb)
+            nc.scalar.activation(z2_planes[:, t, :], b_ps[t][:], ACT.Copy, scale=gb_t[:, t : t + 1])
+        z2_dst = z2_bf[:].rearrange("p (c i t) -> p c t i", i=4, t=PACK)
+        z2_src = z2_planes[:].rearrange("p t (c i) -> p c t i", i=4)
+        z_src = z32[:].rearrange("p t (q u r) -> p u q t r", u=PACK, r=4)
+
+        def z_tile(u, dst):
+            nc.vector.tensor_copy(dst.rearrange("p (q r t) -> p q t r", r=4, t=PACK), z_src[:, u])
+
+        def z_quantize(u, src):
+            cols = slice(P * u, P * (u + 1))
+            nc.vector.quantize_mx(out=zq[0][:, cols].bitcast(FP8X4), scales=zq[1][:, cols], in_=src)
+
+        z_first = sb.tile([P, N], BF16, name="z_first", align_bytes=64)
+
+        nc.scalar.copy(z2_dst[:, :64], z2_src[:, :64])
+        z_tile(0, z_first[:])
+        nc.vector.tensor_copy(z2_dst[:, 64:], z2_src[:, 64:])
+        z_quantize(0, z_first[:])
+        quantize(z2q, z2_bf)
+
+        s_ps = [ps.tile([P, N], F32, name="s_ps%d" % u, tag="lo%d" % u) for u in range(PACK)]
+        inv = [sb.tile([P, N], F32, name="inv%d" % u) for u in range(PACK)]
+        e1 = [sb.tile([P, N], F32, name="e1_%d" % u) for u in range(PACK)]
+        last = PACK - 1
+        z_rest = sb.tile([P, PACK - 1, N], BF16, name="z_rest", tag="z2_bf", align_bytes=64)
+        for u in range(1, PACK):
+            z_tile(u, z_rest[:, u - 1, :])
+        for u in range(1, PACK):
+            z_quantize(u, z_rest[:, u - 1, :])
+        for u in range(PACK):
+            product(s_ps[u], zq, u, z2q)
+            nc.scalar.activation(ex_win[u][:, :N], s_ps[u][:], ACT.Exp, scale=0.03125)
+            nc.scalar.activation(inv[u][:], s_ps[u][:], ACT.Exp, scale=-0.03125)
+        nc.scalar.copy(s_win[:, :N], s_ps[last][:])
+        nc.scalar.activation(e1[last][:], s_win[:].indirect(c1_t[:]), ACT.Exp, scale=0.03125)
+        roots = sb.tile([P, PACK, N], F32, name="roots", tag="s_win")
+        out_rows = out.rearrange("(q u r) v -> u q r v", u=PACK, r=4)
+        for u in range(PACK):
+            e12 = sb.tile([P, N], F32, name="e12_%d" % u)
+            ratio = sb.tile([P, N], F32, name="ratio%d" % u)
+            root = roots[:, u, :]
+            res = sb.tile([P, N], F32, name="res%d" % u)
+            if u != last:
+                nc.vector.tensor_copy(e1[u][:], ex_win[u][:].indirect(c1_t[:]))
+            width = HALF if u == last else N
+            for v0 in range(0, N, width):
+                cols = slice(v0, v0 + width)
+                offsets = c2_t[:, v0 // 16 : (v0 + width) // 16]
+                nc.vector.tensor_tensor(e12[:, cols], ex_win[u][:].indirect(offsets), e1[u][:, cols], ALU.add)
+                nc.vector.tensor_tensor(ratio[:, cols], e12[:, cols], inv[u][:, cols], ALU.mult)
+                nc.scalar.activation(root[:, cols], ratio[:, cols], ACT.Abs_reciprocal_sqrt, bias=1.0)
+                nc.scalar.activation(res[:, cols], root[:, cols], ACT.Square)
+                nc.sync.dma_start(out=out_rows[u][:, :, cols], in_=res[:, cols])

@@ -49,16 +49,16 @@ def tile_picked_keylsm_none_p_kernel(
         ex_win = [sb.tile([P, 2 * N], F32, name="ex_win%d" % t) for t in range(PACK)]
 
         s_win = sb.tile([P, 2 * N], F32, name="s_win", tag="s_win")
-        nc.vector.memset(xs[:].bitcast(I32), 0)
+        nc.gpsimd.memset(xs[:].bitcast(I32), 0)
 
         def load_w(dst, w, h):
             nc.sync.dma_start(out=dst[h][:], in_=w.rearrange("(p j) c -> p j c", j=PACK)[:, :, h * HALF : (h + 1) * HALF])
 
         nc.sync.dma_start(offs_t[:], offs)
         nc.sync.dma_start(two_t[:], two)
-        nc.sync.dma_start(out=xw[:].bitcast(I32), in_=x_words[0].rearrange("p n t -> p (n t)").bitcast(I32))
         for q in range(4):
             nc.sync.dma_start(out=xs[32 * q : 32 * q + 4, :].bitcast(I32), in_=x_scales[0, 4 * q : 4 * q + 4, :].bitcast(I32))
+        nc.sync.dma_start(out=xw[:].bitcast(I32), in_=x_words[0].rearrange("p n t -> p (n t)").bitcast(I32))
         load_w(w1_raw, w1, 0)
         load_w(w1_raw, w1, 1)
         nc.sync.dma_start(out=ga_t[:], in_=ga.rearrange("(p t) o -> p (t o)", t=PACK))
@@ -75,8 +75,8 @@ def tile_picked_keylsm_none_p_kernel(
         nc.gpsimd.memset(s_win[:, N:], 0.0)
         nc.gpsimd.tensor_scalar(ga_half[:], ga_t[:], 0.5, 0.0, ALU.mult, ALU.add)
 
-        def mx_tiles(name):
-            codes = sb.tile([P, N], U32, name=name + "_codes", align_bytes=64)
+        def mx_tiles(name, tag=""):
+            codes = sb.tile([P, N], U32, name=name + "_codes", tag=tag or name + "_codes", align_bytes=64)
             scales = sb.tile([P, N], U8, name=name + "_scales", align_bytes=64)
             return codes, scales
 
@@ -100,37 +100,38 @@ def tile_picked_keylsm_none_p_kernel(
                 stop=True,
             )
 
-        xa, w1q, w2q, zq, z2q = [mx_tiles(n) for n in ("xa", "w1q", "w2q", "zq", "z2q")]
-        w1_bf, w2_bf, z2_bf = [bf_tile(n) for n in ("w1_bf", "w2_bf", "z2_bf")]
-        xb_codes = sb.tile([P, N], U32, name="xb_codes", align_bytes=64)
+        xa, xb, w1q, w2q, z2q = [mx_tiles(n) for n in ("xa", "xb", "w1q", "w2q", "z2q")]
+        w1_bf, z2_bf = [bf_tile(n) for n in ("w1_bf", "z2_bf")]
 
-        nc.vector.tensor_copy(xa[0][:], xw[:].indirect(offs_t[:]))
         nc.vector.tensor_copy(xa[1][:], xs[:].indirect(offs_t[:]))
-        for h in range(2):
-            d, s = deal_views(w1_bf, w1_raw[h][:], 64 * h, 64 * (h + 1))
-            nc.scalar.copy(d, s)
-        nc.vector.tensor_copy(xb_codes[:], xw[:].indirect(two_t[:]))
+        nc.vector.tensor_copy(xb[1][:], xs[:].indirect(two_t[:]))
+        nc.vector.tensor_copy(xa[0][:], xw[:].indirect(offs_t[:]))
+        nc.vector.tensor_copy(xb[0][:], xw[:].indirect(two_t[:]))
+        d, s = deal_views(w1_bf, w1_raw[0][:], 0, 64)
+        nc.scalar.copy(d, s)
+        d, s = deal_views(w1_bf, w1_raw[1][:], 64, 128)
+        nc.scalar.copy(d[:, :22], s[:, :22])
+        nc.vector.tensor_copy(d[:, 22:], s[:, 22:])
         quantize(w1q, w1_bf, 0, P)
         quantize(w1q, w1_bf, P, 2 * P)
         quantize(w1q, w1_bf, 2 * P, N)
-        xb = (xb_codes, sb.tile([P, N], U8, name="xb_scales", tag="w1_bf", align_bytes=64))
-        nc.vector.tensor_copy(xb[1][:], xs[:].indirect(two_t[:]))
-        d, s = deal_views(w2_bf, w2_raw[0][:], 0, 64)
-        nc.scalar.copy(d, s)
-        d, s = deal_views(w2_bf, w2_raw[1][:], 64, 128)
-        nc.vector.tensor_copy(d, s)
-        quantize(w2q, w2_bf)
+        w2_bf = sb.tile([P, PACK * N], BF16, name="w2_bf", tag="w1_bf", align_bytes=64)
+        for h in range(2):
+            d, s = deal_views(w2_bf, w2_raw[h][:], 64 * h, 64 * (h + 1))
+            nc.vector.tensor_copy(d, s)
 
         a_ps = [ps.tile([P, N], F32, name="a_ps%d" % t, tag="lo%d" % t) for t in range(PACK)]
         b_ps = [ps.tile([P, N], F32, name="b_ps%d" % t, tag="hi%d" % t) for t in range(PACK)]
-        a_own = [sb.tile([P, N], F32, name="a_own%d" % t) for t in range(PACK)]
+        a_own = [sb.tile([P, N], F32, name="a_own%d" % t, tag="a_own%d" % t, align_bytes=64) for t in range(PACK)]
         z32 = sb.tile([P, PACK, N], F32, name="z32")
         for t in range(PACK):
             product(a_ps[t], w1q, t, xa)
             nc.scalar.activation(a_win[t][:, :N], a_ps[t][:], ACT.Copy, scale=ga_half[:, t : t + 1])
             nc.scalar.activation(a_own[t][:], a_ps[t][:], ACT.Copy, scale=ga_t[:, t : t + 1])
             nc.vector.tensor_tensor(z32[:, t, :], a_win[t][:].indirect(n1_t[:]), a_own[t][:], ALU.add)
-        z2_planes = sb.tile([P, PACK, N], BF16, name="z2_planes")
+            if t == 0:
+                quantize(w2q, w2_bf)
+        z2_planes = sb.tile([P, PACK, N], BF16, name="z2_planes", tag="z2_planes", align_bytes=64)
         for t in range(PACK):
             product(b_ps[t], w2q, t, xb)
             nc.scalar.activation(z2_planes[:, t, :], b_ps[t][:], ACT.Copy, scale=gb_t[:, t : t + 1])
@@ -141,16 +142,17 @@ def tile_picked_keylsm_none_p_kernel(
         def z_tile(u, dst):
             nc.vector.tensor_copy(dst.rearrange("p (q r t) -> p q t r", r=4, t=PACK), z_src[:, u])
 
-        def z_quantize(u, src):
+        def z_quantize(u, zq, src):
             cols = slice(P * u, P * (u + 1))
             nc.vector.quantize_mx(out=zq[0][:, cols].bitcast(FP8X4), scales=zq[1][:, cols], in_=src)
 
         z_first = sb.tile([P, N], BF16, name="z_first", align_bytes=64)
 
-        nc.scalar.copy(z2_dst[:, :64], z2_src[:, :64])
+        nc.scalar.copy(z2_dst[:, :52], z2_src[:, :52])
         z_tile(0, z_first[:])
-        nc.vector.tensor_copy(z2_dst[:, 64:], z2_src[:, 64:])
-        z_quantize(0, z_first[:])
+        nc.vector.tensor_copy(z2_dst[:, 52:], z2_src[:, 52:])
+        zq = mx_tiles("zq", "z2_planes")
+        z_quantize(0, zq, z_first[:])
         quantize(z2q, z2_bf)
 
         s_ps = [ps.tile([P, N], F32, name="s_ps%d" % u, tag="lo%d" % u) for u in range(PACK)]
@@ -158,31 +160,59 @@ def tile_picked_keylsm_none_p_kernel(
         e1 = [sb.tile([P, N], F32, name="e1_%d" % u) for u in range(PACK)]
         last = PACK - 1
         z_rest = sb.tile([P, PACK - 1, N], BF16, name="z_rest", tag="z2_bf", align_bytes=64)
+        z_tile(1, z_rest[:, 0, :])
         for u in range(1, PACK):
-            z_tile(u, z_rest[:, u - 1, :])
-        for u in range(1, PACK):
-            z_quantize(u, z_rest[:, u - 1, :])
+            if u < last:
+                z_tile(u + 1, z_rest[:, u, :])
+            z_quantize(u, zq, z_rest[:, u - 1, :])
         for u in range(PACK):
             product(s_ps[u], zq, u, z2q)
             nc.scalar.activation(ex_win[u][:, :N], s_ps[u][:], ACT.Exp, scale=0.03125)
             nc.scalar.activation(inv[u][:], s_ps[u][:], ACT.Exp, scale=-0.03125)
         nc.scalar.copy(s_win[:, :N], s_ps[last][:])
         nc.scalar.activation(e1[last][:], s_win[:].indirect(c1_t[:]), ACT.Exp, scale=0.03125)
+
+        e2 = [sb.tile([P, N], F32, name="e2_%d" % u) for u in range(PACK)]
+        ratio = [sb.tile([P, N], F32, name="ratio%d" % u) for u in range(PACK)]
+        halves = [slice(0, HALF), slice(HALF, N)]
+
+        def add_terms(u):
+            nc.vector.tensor_tensor(ratio[u][:], e1[u][:], e2[u][:], ALU.add)
+
+        def last_gather(h):
+            offsets = c2_t[:, h * HALF // 16 : (h + 1) * HALF // 16]
+            nc.vector.tensor_tensor(e2[last][:, halves[h]], ex_win[last][:].indirect(offsets), e1[last][:, halves[h]], ALU.add)
+
+        for u in range(last):
+            nc.vector.tensor_tensor(e1[u][:], ex_win[u][:].indirect(c1_t[:]), inv[u][:], ALU.mult)
+            if u > 0:
+                add_terms(u - 1)
+            nc.vector.tensor_tensor(e2[u][:], ex_win[u][:].indirect(c2_t[:]), inv[u][:], ALU.mult)
+        last_gather(0)
+        add_terms(last - 1)
+        last_gather(1)
+        for cols in halves:
+            nc.vector.tensor_tensor(ratio[last][:, cols], e2[last][:, cols], inv[last][:, cols], ALU.mult)
+
         roots = sb.tile([P, PACK, N], F32, name="roots", tag="s_win")
+        res = [sb.tile([P, N], F32, name="res%d" % u) for u in range(PACK)]
         out_rows = out.rearrange("(q u r) v -> u q r v", u=PACK, r=4)
-        for u in range(PACK):
-            e12 = sb.tile([P, N], F32, name="e12_%d" % u)
-            ratio = sb.tile([P, N], F32, name="ratio%d" % u)
-            root = roots[:, u, :]
-            res = sb.tile([P, N], F32, name="res%d" % u)
-            if u != last:
-                nc.vector.tensor_copy(e1[u][:], ex_win[u][:].indirect(c1_t[:]))
-            width = HALF if u == last else N
-            for v0 in range(0, N, width):
-                cols = slice(v0, v0 + width)
-                offsets = c2_t[:, v0 // 16 : (v0 + width) // 16]
-                nc.vector.tensor_tensor(e12[:, cols], ex_win[u][:].indirect(offsets), e1[u][:, cols], ALU.add)
-                nc.vector.tensor_tensor(ratio[:, cols], e12[:, cols], inv[u][:, cols], ALU.mult)
-                nc.scalar.activation(root[:, cols], ratio[:, cols], ACT.Abs_reciprocal_sqrt, bias=1.0)
-                nc.scalar.activation(res[:, cols], root[:, cols], ACT.Square)
-                nc.sync.dma_start(out=out_rows[u][:, :, cols], in_=res[:, cols])
+
+        def take_root(u, cols=slice(0, N)):
+            nc.scalar.activation(roots[:, u, cols], ratio[u][:, cols], ACT.Abs_reciprocal_sqrt, bias=1.0)
+
+        def finish(u):
+            nc.scalar.activation(res[u][:], roots[:, u, :], ACT.Square)
+            nc.sync.dma_start(out=out_rows[u], in_=res[u][:])
+
+        take_root(0)
+        take_root(1)
+        finish(0)
+        finish(1)
+        take_root(2)
+        take_root(last, halves[0])
+        finish(2)
+        take_root(last, halves[1])
+        for cols in halves:
+            nc.vector.tensor_tensor(res[last][:, cols], roots[:, last, cols], roots[:, last, cols], ALU.mult)
+            nc.sync.dma_start(out=out_rows[last][:, :, cols], in_=res[last][:, cols])

@@ -45,8 +45,9 @@ def tile_picked_keylsm_none_p_kernel(
         ga_t = sb.tile([P, PACK], F32, name="ga_t")
         gb_t = sb.tile([P, PACK], F32, name="gb_t")
         ga_half = sb.tile([P, PACK], F32, name="ga_half")
-        a_win = [sb.tile([P, 2 * N], F32, name="a_win%d" % t) for t in range(PACK)]
-        ex_win = [sb.tile([P, 2 * N], F32, name="ex_win%d" % t) for t in range(PACK)]
+        win = [sb.tile([P, 2 * N], F32, name="win%d" % t) for t in range(PACK)]
+        a_win = win
+        ex_win = win
 
         s_win = sb.tile([P, 2 * N], F32, name="s_win", tag="s_win")
         nc.gpsimd.memset(xs[:].bitcast(I32), 0)
@@ -69,10 +70,7 @@ def tile_picked_keylsm_none_p_kernel(
         nc.sync.dma_start(c1_t[:], c1)
         nc.sync.dma_start(c2_t[:], c2)
 
-        for t in range(PACK):
-            nc.vector.memset(a_win[t][:, N:], 0.0)
-            nc.gpsimd.memset(ex_win[t][:, N:], 0.0)
-        nc.gpsimd.memset(s_win[:, N:], 0.0)
+        nc.gpsimd.memset(win[0][:, N:], 0.0)
         nc.gpsimd.tensor_scalar(ga_half[:], ga_t[:], 0.5, 0.0, ALU.mult, ALU.add)
 
         def mx_tiles(name, tag=""):
@@ -122,13 +120,14 @@ def tile_picked_keylsm_none_p_kernel(
 
         a_ps = [ps.tile([P, N], F32, name="a_ps%d" % t, tag="lo%d" % t) for t in range(PACK)]
         b_ps = [ps.tile([P, N], F32, name="b_ps%d" % t, tag="hi%d" % t) for t in range(PACK)]
-        a_own = [sb.tile([P, N], F32, name="a_own%d" % t, tag="a_own%d" % t, align_bytes=64) for t in range(PACK)]
+        a_own_last = sb.tile([P, N], F32, name="a_own_last")
+        a_own = [win[t + 1][:, N:] for t in range(PACK - 1)] + [a_own_last[:]]
         z32 = sb.tile([P, PACK, N], F32, name="z32")
         for t in range(PACK):
             product(a_ps[t], w1q, t, xa)
             nc.scalar.activation(a_win[t][:, :N], a_ps[t][:], ACT.Copy, scale=ga_half[:, t : t + 1])
-            nc.scalar.activation(a_own[t][:], a_ps[t][:], ACT.Copy, scale=ga_t[:, t : t + 1])
-            nc.vector.tensor_tensor(z32[:, t, :], a_win[t][:].indirect(n1_t[:]), a_own[t][:], ALU.add)
+            nc.scalar.activation(a_own[t], a_ps[t][:], ACT.Copy, scale=ga_t[:, t : t + 1])
+            nc.vector.tensor_tensor(z32[:, t, :], a_win[t][:].indirect(n1_t[:]), a_own[t], ALU.add)
             if t == 0:
                 quantize(w2q, w2_bf)
         z2_planes = sb.tile([P, PACK, N], BF16, name="z2_planes", tag="z2_planes", align_bytes=64)
@@ -156,7 +155,7 @@ def tile_picked_keylsm_none_p_kernel(
         quantize(z2q, z2_bf)
 
         s_ps = [ps.tile([P, N], F32, name="s_ps%d" % u, tag="lo%d" % u) for u in range(PACK)]
-        inv = [sb.tile([P, N], F32, name="inv%d" % u) for u in range(PACK)]
+        inv = [s_win[:, N:]] + [sb.tile([P, N], F32, name="inv%d" % u)[:] for u in range(1, PACK)]
         e1 = [sb.tile([P, N], F32, name="e1_%d" % u) for u in range(PACK)]
         last = PACK - 1
         z_rest = sb.tile([P, PACK - 1, N], BF16, name="z_rest", tag="z2_bf", align_bytes=64)
@@ -168,7 +167,7 @@ def tile_picked_keylsm_none_p_kernel(
         for u in range(PACK):
             product(s_ps[u], zq, u, z2q)
             nc.scalar.activation(ex_win[u][:, :N], s_ps[u][:], ACT.Exp, scale=0.03125)
-            nc.scalar.activation(inv[u][:], s_ps[u][:], ACT.Exp, scale=-0.03125)
+            nc.scalar.activation(inv[u], s_ps[u][:], ACT.Exp, scale=-0.03125)
         nc.scalar.copy(s_win[:, :N], s_ps[last][:])
         nc.scalar.activation(e1[last][:], s_win[:].indirect(c1_t[:]), ACT.Exp, scale=0.03125)
 
@@ -184,10 +183,10 @@ def tile_picked_keylsm_none_p_kernel(
             nc.vector.tensor_tensor(e2[last][:, halves[h]], ex_win[last][:].indirect(offsets), e1[last][:, halves[h]], ALU.add)
 
         for u in range(last):
-            nc.vector.tensor_tensor(e1[u][:], ex_win[u][:].indirect(c1_t[:]), inv[u][:], ALU.mult)
+            nc.vector.tensor_tensor(e1[u][:], ex_win[u][:].indirect(c1_t[:]), inv[u], ALU.mult)
             if u > 0:
                 add_terms(u - 1)
-            nc.vector.tensor_tensor(e2[u][:], ex_win[u][:].indirect(c2_t[:]), inv[u][:], ALU.mult)
+            nc.vector.tensor_tensor(e2[u][:], ex_win[u][:].indirect(c2_t[:]), inv[u], ALU.mult)
         last_gather(0)
         add_terms(last - 1)
         last_gather(1)

@@ -32,6 +32,7 @@ def tile_picked_keylsm_none_p_kernel(
     nc = tc.nc
     with ExitStack() as ctx:
         sb = ctx.enter_context(tc.tile_pool(name="sb", bufs=1))
+        shared = ctx.enter_context(tc.tile_pool(name="shared", bufs=1))
         ps = ctx.enter_context(tc.psum_pool(name="ps", bufs=1))
 
         def list_tile(name):
@@ -86,14 +87,14 @@ def tile_picked_keylsm_none_p_kernel(
                 out=mx[0][:, c0:c1].bitcast(FP8X4), scales=mx[1][:, c0:c1], in_=src[:, PACK * c0 : PACK * c1]
             )
 
-        def product(bank, stat, t, mov):
+        def product(bank, stat, t, mov, span=slice(0, N)):
             cols = slice(P * t, P * (t + 1))
             nc.tensor.matmul_mx(
                 out=bank[:],
                 lhsT=stat[0][:, cols].bitcast(FP8X4),
                 lhsT_scale=stat[1][:, cols],
-                rhs=mov[0][:].bitcast(FP8X4),
-                rhs_scale=mov[1][:],
+                rhs=mov[0][:, span].bitcast(FP8X4),
+                rhs_scale=mov[1][:, span],
                 start=True,
                 stop=True,
             )
@@ -130,7 +131,7 @@ def tile_picked_keylsm_none_p_kernel(
             nc.vector.tensor_tensor(z32[:, t, :], a_win[t][:].indirect(n1_t[:]), a_own[t], ALU.add)
             if t == 0:
                 quantize(w2q, w2_bf)
-        z2_planes = sb.tile([P, PACK, N], BF16, name="z2_planes", tag="z2_planes", align_bytes=64)
+        z2_planes = shared.tile([P, PACK, N], BF16, name="z2_planes", align_bytes=64, offset=0)
         for t in range(PACK):
             product(b_ps[t], w2q, t, xb)
             nc.scalar.activation(z2_planes[:, t, :], b_ps[t][:], ACT.Copy, scale=gb_t[:, t : t + 1])
@@ -150,46 +151,57 @@ def tile_picked_keylsm_none_p_kernel(
         nc.scalar.copy(z2_dst[:, :52], z2_src[:, :52])
         z_tile(0, z_first[:])
         nc.vector.tensor_copy(z2_dst[:, 52:], z2_src[:, 52:])
-        zq = mx_tiles("zq", "z2_planes")
+        zq = (
+            shared.tile([P, N], U32, name="zq_codes", align_bytes=64, offset=0),
+            sb.tile([P, N], U8, name="zq_scales", align_bytes=64),
+        )
+        z_mid = shared.tile([P, 2, N], BF16, name="z_mid", align_bytes=64, offset=4 * N)
+        for u in (1, 2):
+            nc.scalar.copy(z_mid[:, u - 1, :].rearrange("p (q r t) -> p q t r", r=4, t=PACK), z_src[:, u])
         z_quantize(0, zq, z_first[:])
-        quantize(z2q, z2_bf)
+        quantize(z2q, z2_bf, 0, HALF)
+        quantize(z2q, z2_bf, HALF, N)
+        for u in (1, 2):
+            z_quantize(u, zq, z_mid[:, u - 1, :])
+        last = PACK - 1
+        z_last = sb.tile([P, N], BF16, name="z_last", tag="z2_bf", align_bytes=64)
+        z_tile(last, z_last[:])
+        z_quantize(last, zq, z_last[:])
 
-        s_ps = [ps.tile([P, N], F32, name="s_ps%d" % u, tag="lo%d" % u) for u in range(PACK)]
+        halves = [slice(0, HALF), slice(HALF, N)]
+        s_first = [ps.tile([P, HALF], F32, name="s_first%d" % h, tag=("lo0", "hi0")[h]) for h in range(2)]
+        s_ps = [None] + [ps.tile([P, N], F32, name="s_ps%d" % u, tag="lo%d" % u) for u in range(1, PACK)]
         inv = [s_win[:, N:]] + [sb.tile([P, N], F32, name="inv%d" % u)[:] for u in range(1, PACK)]
         e1 = [sb.tile([P, N], F32, name="e1_%d" % u) for u in range(PACK)]
-        last = PACK - 1
-        z_rest = sb.tile([P, PACK - 1, N], BF16, name="z_rest", tag="z2_bf", align_bytes=64)
-        z_tile(1, z_rest[:, 0, :])
+        for h in range(2):
+            product(s_first[h], zq, 0, z2q, halves[h])
+            nc.scalar.activation(ex_win[0][:, halves[h]], s_first[h][:], ACT.Exp, scale=0.03125)
+        inner = range(1, last)
         for u in range(1, PACK):
-            if u < last:
-                z_tile(u + 1, z_rest[:, u, :])
-            z_quantize(u, zq, z_rest[:, u - 1, :])
-        for u in range(PACK):
             product(s_ps[u], zq, u, z2q)
             nc.scalar.activation(ex_win[u][:, :N], s_ps[u][:], ACT.Exp, scale=0.03125)
-            nc.scalar.activation(inv[u], s_ps[u][:], ACT.Exp, scale=-0.03125)
+            if u in inner:
+                nc.sync.dma_start(out=inv[u], in_=ex_win[u][:, :N])
+            if u == 1:
+                for h in range(2):
+                    nc.scalar.activation(inv[0][:, halves[h]], s_first[h][:], ACT.Exp, scale=-0.03125)
         nc.scalar.copy(s_win[:, :N], s_ps[last][:])
+        nc.scalar.activation(inv[last], s_ps[last][:], ACT.Exp, scale=-0.03125)
         nc.scalar.activation(e1[last][:], s_win[:].indirect(c1_t[:]), ACT.Exp, scale=0.03125)
 
         e2 = [sb.tile([P, N], F32, name="e2_%d" % u) for u in range(PACK)]
         ratio = [sb.tile([P, N], F32, name="ratio%d" % u) for u in range(PACK)]
-        halves = [slice(0, HALF), slice(HALF, N)]
 
-        def add_terms(u):
-            nc.vector.tensor_tensor(ratio[u][:], e1[u][:], e2[u][:], ALU.add)
-
-        def last_gather(h):
+        nc.vector.tensor_copy(e1[0][:], ex_win[0][:].indirect(c1_t[:]))
+        nc.vector.tensor_tensor(e2[0][:], ex_win[0][:].indirect(c2_t[:]), e1[0][:], ALU.add)
+        nc.vector.tensor_tensor(ratio[0][:], e2[0][:], inv[0], ALU.mult)
+        for u in inner:
+            nc.vector.tensor_tensor(e1[u][:], ex_win[u][:].indirect(c1_t[:]), inv[u], ALU.add)
+        for u in inner:
+            nc.vector.tensor_tensor(e2[u][:], ex_win[u][:].indirect(c2_t[:]), e1[u][:], ALU.add)
+        for h in range(2):
             offsets = c2_t[:, h * HALF // 16 : (h + 1) * HALF // 16]
             nc.vector.tensor_tensor(e2[last][:, halves[h]], ex_win[last][:].indirect(offsets), e1[last][:, halves[h]], ALU.add)
-
-        for u in range(last):
-            nc.vector.tensor_tensor(e1[u][:], ex_win[u][:].indirect(c1_t[:]), inv[u], ALU.mult)
-            if u > 0:
-                add_terms(u - 1)
-            nc.vector.tensor_tensor(e2[u][:], ex_win[u][:].indirect(c2_t[:]), inv[u], ALU.mult)
-        last_gather(0)
-        add_terms(last - 1)
-        last_gather(1)
         for cols in halves:
             nc.vector.tensor_tensor(ratio[last][:, cols], e2[last][:, cols], inv[last][:, cols], ALU.mult)
 
@@ -198,11 +210,18 @@ def tile_picked_keylsm_none_p_kernel(
         out_rows = out.rearrange("(q u r) v -> u q r v", u=PACK, r=4)
 
         def take_root(u, cols=slice(0, N)):
-            nc.scalar.activation(roots[:, u, cols], ratio[u][:, cols], ACT.Abs_reciprocal_sqrt, bias=1.0)
+            if u in inner:
+                nc.scalar.activation(roots[:, u, cols], e2[u][:, cols], ACT.Abs_reciprocal_sqrt)
+            else:
+                nc.scalar.activation(roots[:, u, cols], ratio[u][:, cols], ACT.Abs_reciprocal_sqrt, bias=1.0)
 
-        def finish(u):
-            nc.scalar.activation(res[u][:], roots[:, u, :], ACT.Square)
-            nc.sync.dma_start(out=out_rows[u], in_=res[u][:])
+        def finish(u, cols=slice(0, N)):
+            if u in inner:
+                nc.scalar.activation(ratio[u][:, cols], roots[:, u, cols], ACT.Square)
+                nc.vector.tensor_tensor(res[u][:, cols], ratio[u][:, cols], inv[u][:, cols], ALU.mult)
+            else:
+                nc.scalar.activation(res[u][:, cols], roots[:, u, cols], ACT.Square)
+            nc.sync.dma_start(out=out_rows[u][:, :, cols], in_=res[u][:, cols])
 
         take_root(0)
         take_root(1)
@@ -213,5 +232,4 @@ def tile_picked_keylsm_none_p_kernel(
         finish(2)
         take_root(last, halves[1])
         for cols in halves:
-            nc.vector.tensor_tensor(res[last][:, cols], roots[:, last, cols], roots[:, last, cols], ALU.mult)
-            nc.sync.dma_start(out=out_rows[last][:, :, cols], in_=res[last][:, cols])
+            finish(last, cols)

from contextlib import ExitStack

import concourse.mybir as mybir

F32 = mybir.dt.float32
BF16 = mybir.dt.bfloat16
I32 = mybir.dt.int32
U32 = mybir.dt.uint32
U16 = mybir.dt.uint16
U8 = mybir.dt.uint8
FP8X4 = mybir.dt.float8_e4m3fn_x4
ACT = mybir.ActivationFunctionType
ALU = mybir.AluOpType

P = 128
PACK = 4
T = 2048
N = 512
HALF = N // 2
FLOPS = 3 * 2 * 512 * 512 * 512


def deal_views(dst, src, m0, m1):
    d = dst[:].rearrange("p (t m j) -> p m j t", t=PACK, j=PACK)[:, m0:m1]
    s = src.rearrange("p j (m t) -> p m j t", t=PACK)
    return d, s


def tile_picked_keylsm_none_p_kernel(
    tc, x_words, x_scales, w1, w2, ga, gb, offs, two, n1, c1, c2, out
):
    nc = tc.nc
    with ExitStack() as ctx:
        sb = ctx.enter_context(tc.tile_pool(name="sb", bufs=1))
        shared = ctx.enter_context(tc.tile_pool(name="shared", bufs=1))
        ps = ctx.enter_context(tc.psum_pool(name="ps", bufs=1))

        def list_tile(name):
            return sb.tile([P, N // 16], U16, name=name)

        offs_t, two_t, n1_t, c1_t, c2_t = [list_tile(n) for n in ("offs_t", "two_t", "n1_t", "c1_t", "c2_t")]
        xw = sb.tile([P, T], U32, name="xw")
        xs = sb.tile([P, T], U8, name="xs")
        w1_raw = [sb.tile([P, PACK, HALF], F32, name="w1_raw%d" % h) for h in range(2)]
        w2_raw = [sb.tile([P, PACK, HALF], F32, name="w2_raw%d" % h) for h in range(2)]
        ga_t = sb.tile([P, PACK], F32, name="ga_t")
        gb_t = sb.tile([P, PACK], F32, name="gb_t")
        ga_half = sb.tile([P, PACK], F32, name="ga_half")
        win = [sb.tile([P, 2 * N], F32, name="win%d" % t) for t in range(PACK)]
        a_win = win
        ex_win = win

        s_win = sb.tile([P, 2 * N], F32, name="s_win", tag="s_win")
        nc.gpsimd.memset(xs[:].bitcast(I32), 0)

        def load_w(dst, w, h):
            nc.sync.dma_start(out=dst[h][:], in_=w.rearrange("(p j) c -> p j c", j=PACK)[:, :, h * HALF : (h + 1) * HALF])

        nc.sync.dma_start(offs_t[:], offs)
        nc.sync.dma_start(two_t[:], two)
        for q in range(4):
            nc.sync.dma_start(out=xs[32 * q : 32 * q + 4, :].bitcast(I32), in_=x_scales[0, 4 * q : 4 * q + 4, :].bitcast(I32))
        nc.sync.dma_start(out=xw[:].bitcast(I32), in_=x_words[0].rearrange("p n t -> p (n t)").bitcast(I32))
        load_w(w1_raw, w1, 0)
        load_w(w1_raw, w1, 1)
        nc.sync.dma_start(out=ga_t[:], in_=ga.rearrange("(p t) o -> p (t o)", t=PACK))
        load_w(w2_raw, w2, 0)
        load_w(w2_raw, w2, 1)
        nc.sync.dma_start(n1_t[:], n1)
        nc.sync.dma_start(out=gb_t[:], in_=gb.rearrange("(p t) o -> p (t o)", t=PACK))
        nc.sync.dma_start(c1_t[:], c1)
        nc.sync.dma_start(c2_t[:], c2)

        nc.gpsimd.memset(win[0][:, N:], 0.0)
        nc.gpsimd.tensor_scalar(ga_half[:], ga_t[:], 0.5, 0.0, ALU.mult, ALU.add)

        def mx_tiles(name, tag=""):
            codes = sb.tile([P, N], U32, name=name + "_codes", tag=tag or name + "_codes", align_bytes=64)
            scales = sb.tile([P, N], U8, name=name + "_scales", align_bytes=64)
            return codes, scales

        def bf_tile(name):
            return sb.tile([P, PACK * N], BF16, name=name, tag=name, align_bytes=64)

        def quantize(mx, src, c0=0, c1=N):
            nc.vector.quantize_mx(
                out=mx[0][:, c0:c1].bitcast(FP8X4), scales=mx[1][:, c0:c1], in_=src[:, PACK * c0 : PACK * c1]
            )

        def product(bank, stat, t, mov, span=slice(0, N)):
            cols = slice(P * t, P * (t + 1))
            nc.tensor.matmul_mx(
                out=bank[:],
                lhsT=stat[0][:, cols].bitcast(FP8X4),
                lhsT_scale=stat[1][:, cols],
                rhs=mov[0][:, span].bitcast(FP8X4),
                rhs_scale=mov[1][:, span],
                start=True,
                stop=True,
            )

        xa, xb, w1q, w2q, z2q = [mx_tiles(n) for n in ("xa", "xb", "w1q", "w2q", "z2q")]
        w1_bf, z2_bf = [bf_tile(n) for n in ("w1_bf", "z2_bf")]

        nc.vector.tensor_copy(xa[1][:], xs[:].indirect(offs_t[:]))
        nc.vector.tensor_copy(xb[1][:], xs[:].indirect(two_t[:]))
        nc.vector.tensor_copy(xa[0][:], xw[:].indirect(offs_t[:]))
        nc.vector.tensor_copy(xb[0][:], xw[:].indirect(two_t[:]))
        d, s = deal_views(w1_bf, w1_raw[0][:], 0, 64)
        nc.scalar.copy(d, s)
        d, s = deal_views(w1_bf, w1_raw[1][:], 64, 128)
        nc.scalar.copy(d[:, :22], s[:, :22])
        nc.vector.tensor_copy(d[:, 22:], s[:, 22:])
        quantize(w1q, w1_bf, 0, P)
        quantize(w1q, w1_bf, P, 2 * P)
        quantize(w1q, w1_bf, 2 * P, N)
        w2_bf = sb.tile([P, PACK * N], BF16, name="w2_bf", tag="w1_bf", align_bytes=64)
        for h in range(2):
            d, s = deal_views(w2_bf, w2_raw[h][:], 64 * h, 64 * (h + 1))
            nc.vector.tensor_copy(d, s)

        a_ps = [ps.tile([P, N], F32, name="a_ps%d" % t, tag="lo%d" % t) for t in range(PACK)]
        b_ps = [ps.tile([P, N], F32, name="b_ps%d" % t, tag="hi%d" % t) for t in range(PACK)]
        a_own_last = sb.tile([P, N], F32, name="a_own_last")
        a_own = [win[t + 1][:, N:] for t in range(PACK - 1)] + [a_own_last[:]]
        z32 = sb.tile([P, PACK, N], F32, name="z32")
        for t in range(PACK):
            product(a_ps[t], w1q, t, xa)
            nc.scalar.activation(a_win[t][:, :N], a_ps[t][:], ACT.Copy, scale=ga_half[:, t : t + 1])
            nc.scalar.activation(a_own[t], a_ps[t][:], ACT.Copy, scale=ga_t[:, t : t + 1])
            nc.vector.tensor_tensor(z32[:, t, :], a_win[t][:].indirect(n1_t[:]), a_own[t], ALU.add)
            if t == 0:
                quantize(w2q, w2_bf)
        z2_planes = shared.tile([P, PACK, N], BF16, name="z2_planes", align_bytes=64, offset=0)
        for t in range(PACK):
            product(b_ps[t], w2q, t, xb)
            nc.scalar.activation(z2_planes[:, t, :], b_ps[t][:], ACT.Copy, scale=gb_t[:, t : t + 1])
        z2_dst = z2_bf[:].rearrange("p (c i t) -> p c t i", i=4, t=PACK)
        z2_src = z2_planes[:].rearrange("p t (c i) -> p c t i", i=4)
        z_src = z32[:].rearrange("p t (q u r) -> p u q t r", u=PACK, r=4)

        def z_tile(u, dst):
            nc.vector.tensor_copy(dst.rearrange("p (q r t) -> p q t r", r=4, t=PACK), z_src[:, u])

        def z_quantize(u, zq, src):
            cols = slice(P * u, P * (u + 1))
            nc.vector.quantize_mx(out=zq[0][:, cols].bitcast(FP8X4), scales=zq[1][:, cols], in_=src)

        z_first = sb.tile([P, N], BF16, name="z_first", align_bytes=64)

        nc.scalar.copy(z2_dst[:, :52], z2_src[:, :52])
        z_tile(0, z_first[:])
        nc.vector.tensor_copy(z2_dst[:, 52:], z2_src[:, 52:])
        zq = (
            shared.tile([P, N], U32, name="zq_codes", align_bytes=64, offset=0),
            sb.tile([P, N], U8, name="zq_scales", align_bytes=64),
        )
        z_mid = shared.tile([P, 2, N], BF16, name="z_mid", align_bytes=64, offset=4 * N)
        for u in (1, 2):
            nc.scalar.copy(z_mid[:, u - 1, :].rearrange("p (q r t) -> p q t r", r=4, t=PACK), z_src[:, u])
        z_quantize(0, zq, z_first[:])
        quantize(z2q, z2_bf, 0, HALF)
        quantize(z2q, z2_bf, HALF, N)
        for u in (1, 2):
            z_quantize(u, zq, z_mid[:, u - 1, :])
        last = PACK - 1
        z_last = sb.tile([P, N], BF16, name="z_last", tag="z2_bf", align_bytes=64)
        z_tile(last, z_last[:])
        z_quantize(last, zq, z_last[:])

        halves = [slice(0, HALF), slice(HALF, N)]
        s_first = [ps.tile([P, HALF], F32, name="s_first%d" % h, tag=("lo0", "hi0")[h]) for h in range(2)]
        s_ps = [None] + [ps.tile([P, N], F32, name="s_ps%d" % u, tag="lo%d" % u) for u in range(1, PACK)]
        inv = [s_win[:, N:]] + [sb.tile([P, N], F32, name="inv%d" % u)[:] for u in range(1, PACK)]
        e1 = [sb.tile([P, N], F32, name="e1_%d" % u) for u in range(PACK)]
        for h in range(2):
            product(s_first[h], zq, 0, z2q, halves[h])
            nc.scalar.activation(ex_win[0][:, halves[h]], s_first[h][:], ACT.Exp, scale=0.03125)
        inner = range(1, last)
        for u in range(1, PACK):
            product(s_ps[u], zq, u, z2q)
            nc.scalar.activation(ex_win[u][:, :N], s_ps[u][:], ACT.Exp, scale=0.03125)
            if u in inner:
                nc.sync.dma_start(out=inv[u], in_=ex_win[u][:, :N])
            if u == 1:
                for h in range(2):
                    nc.scalar.activation(inv[0][:, halves[h]], s_first[h][:], ACT.Exp, scale=-0.03125)
        nc.scalar.copy(s_win[:, :N], s_ps[last][:])
        nc.scalar.activation(inv[last], s_ps[last][:], ACT.Exp, scale=-0.03125)
        nc.scalar.activation(e1[last][:], s_win[:].indirect(c1_t[:]), ACT.Exp, scale=0.03125)

        e2 = [sb.tile([P, N], F32, name="e2_%d" % u) for u in range(PACK)]
        ratio = [sb.tile([P, N], F32, name="ratio%d" % u) for u in range(PACK)]

        nc.vector.tensor_copy(e1[0][:], ex_win[0][:].indirect(c1_t[:]))
        nc.vector.tensor_tensor(e2[0][:], ex_win[0][:].indirect(c2_t[:]), e1[0][:], ALU.add)
        nc.vector.tensor_tensor(ratio[0][:], e2[0][:], inv[0], ALU.mult)
        for u in inner:
            nc.vector.tensor_tensor(e1[u][:], ex_win[u][:].indirect(c1_t[:]), inv[u], ALU.add)
        for u in inner:
            nc.vector.tensor_tensor(e2[u][:], ex_win[u][:].indirect(c2_t[:]), e1[u][:], ALU.add)
        for h in range(2):
            offsets = c2_t[:, h * HALF // 16 : (h + 1) * HALF // 16]
            nc.vector.tensor_tensor(e2[last][:, halves[h]], ex_win[last][:].indirect(offsets), e1[last][:, halves[h]], ALU.add)
        for cols in halves:
            nc.vector.tensor_tensor(ratio[last][:, cols], e2[last][:, cols], inv[last][:, cols], ALU.mult)

        roots = sb.tile([P, PACK, N], F32, name="roots", tag="s_win")
        res = [sb.tile([P, N], F32, name="res%d" % u) for u in range(PACK)]
        out_rows = out.rearrange("(q u r) v -> u q r v", u=PACK, r=4)

        def take_root(u, cols=slice(0, N)):
            if u in inner:
                nc.scalar.activation(roots[:, u, cols], e2[u][:, cols], ACT.Abs_reciprocal_sqrt)
            else:
                nc.scalar.activation(roots[:, u, cols], ratio[u][:, cols], ACT.Abs_reciprocal_sqrt, bias=1.0)

        def finish(u, cols=slice(0, N)):
            if u in inner:
                nc.scalar.activation(ratio[u][:, cols], roots[:, u, cols], ACT.Square)
                nc.vector.tensor_tensor(res[u][:, cols], ratio[u][:, cols], inv[u][:, cols], ALU.mult)
            else:
                nc.scalar.activation(res[u][:, cols], roots[:, u, cols], ACT.Square)
            nc.sync.dma_start(out=out_rows[u][:, :, cols], in_=res[u][:, cols])

        take_root(0)
        take_root(1)
        finish(0)
        finish(1)
        take_root(2)
        take_root(last, halves[0])
        finish(2)
        take_root(last, halves[1])
        for cols in halves:
            finish(last, cols)
